import numpy as np, ml_dtypes
CORES = [37,45,53,61,69,109,117,125]
N = 8
NB, TK, FT = 8, 64, 2
def setup_inputs(rng):
    return {"x": rng.standard_normal((N, NB, 128, TK), dtype=np.float32).astype(ml_dtypes.bfloat16), "w1": (rng.standard_normal((N, 128, FT * 128), dtype=np.float32) / 8).astype(ml_dtypes.bfloat16), "w2": (rng.standard_normal((N, 128, FT * 128), dtype=np.float32) / np.float32(8 * np.sqrt(FT))).astype(ml_dtypes.bfloat16)}
def setup_inputs_big(rng):
    d = setup_inputs(rng)
    for k in ("x",): d[k] = (d[k].astype(np.float32) * 1048576.0).astype(d[k].dtype)
    return d
def setup_inputs_small(rng):
    d = setup_inputs(rng)
    for k in ("x",): d[k] = (d[k].astype(np.float32) * (1 / 1048576.0)).astype(d[k].dtype)
    return d
def reference(x, w1, w2):
    W1, W2 = w1.astype(np.float64), w2.astype(np.float64)
    a = x[0].astype(np.float64)
    for s in range(N):
        a = sum(np.einsum("kf,bkn->bfn", W2[s][:, 128 * f:128 * f + 128], np.maximum(np.einsum("kf,bkn->bfn", W1[s][:, 128 * f:128 * f + 128], a), 0.0)) for f in range(FT))
    y = np.full(x.shape, np.nan, ml_dtypes.bfloat16)
    y[N - 1] = a.astype(ml_dtypes.bfloat16)
    return {"y": y}

@@ -1,0 +1,242 @@
+from concourse.bass import DstId, RemoteDMATransfer
+from concourse.mybir import AluOpType
+
+NB, TK, FT = 8, 64, 2
+NST = 8
+COLS = NB * TK
+HALF = FT * 128
+WID = 2 * HALF
+C_HELP = 96
+NCH = 5
+
+SCRATCH = {
+    "wall": ("sbuf", [128, NST * WID], "bfloat16"),
+    "xin": ("sbuf", [128, COLS], "bfloat16"),
+    "act": ("sbuf", [128, COLS], "bfloat16"),
+    "hid": ("sbuf", [128, FT * COLS], "bfloat16"),
+    "out": ("sbuf", [128, COLS], "bfloat16"),
+    "zero": ("sbuf", [128, 512], "float32"),
+}
+for _k in range(NCH):
+    SCRATCH["ps%d" % _k] = ("psum", [128, 512], "float32")
+
+SEMAPHORES = (["wa%d" % s for s in range(NST)] + ["wb%d" % s for s in range(NST)]
+              + ["xb%d" % m for m in range(NB)]
+              + ["t%d" % k for k in range(NCH)] + ["v%d" % k for k in range(NCH)]
+              + ["res%d" % q for q in range(1, 4)]
+              + ["ain", "lsem", "st", "zs"])
+
+
+def rank_program(g, core, T, topo):
+    ranks = list(T.cores)
+    first, last = ranks[0], ranks[-1]
+    every = range(topo.CHIPS * topo.CORES_PER_CHIP)
+
+    comp = [last] + [r for r in ranks[1:-1] if topo.may_write(r, last)]
+    width = [COLS - C_HELP * (len(comp) - 1)] + [C_HELP] * (len(comp) - 1)
+    offs = [sum(width[:q]) for q in range(len(comp))]
+
+    def port_cores(r):
+        c = [k for k in every if topo.chip(k) == topo.chip(r) and k not in ranks
+             and all(topo.may_write(k, d) for d in comp)]
+        return ([k for k in c if topo.die(k) == topo.die(r)], [k for k in c if topo.die(k) != topo.die(r)])
+
+    near, far = port_cores(first)
+    a_relay = [far[0], near[0], far[1], near[1]]
+    w_jobs = {}
+    w_relay = {}
+    for s in range(1, NST):
+        if ranks[s] in comp:
+            continue
+        nr, fr = port_cores(ranks[s])
+        w_relay[s] = [[fr[0], nr[1]], [nr[0], fr[1]]]
+        for h in range(2):
+            for p in range(2):
+                w_jobs[w_relay[s][h][p]] = (s, h, comp[2 * p:2 * p + 2])
+
+    waited = {}
+    left = [0]
+
+    def wait(q, qname, sem, val):
+        if val > waited.get((qname, sem), 0):
+            waited[(qname, sem)] = val
+            q.wait_ge(T.sem[sem], val)
+
+    def gwait(sem, val):
+        wait(g, "g", sem, val)
+
+    def engines(dsts):
+        m = topo.mask(core, dsts[0])
+        for d in dsts[1:]:
+            m &= topo.mask(core, d)
+        return [e for e in range(m.bit_length()) if (m >> e) & 1]
+
+    def bits(es):
+        m = 0
+        for e in es:
+            m |= 1 << e
+        return m
+
+    def transfer(ap, dsts, es, sem):
+        ids = []
+        for d in dsts:
+            a = topo.addr(d)
+            ids.append(DstId(rid=a[0], pnc=a[1]))
+        left[0] += len(es)
+        return RemoteDMATransfer(dst_ids=ids, dma_engine_mask=bits(es), remote_sem=T.sem[sem],
+                                 srcs=[ap], dsts=[ap for d in dsts], alu_op=0)
+
+    def send(trs):
+        g.remote_dma_fused(trs, local_sem=T.sem.lsem)
+
+    def send_one(ap, dst, es, sem):
+        a = topo.addr(dst)
+        left[0] += len(es)
+        g.remote_dma(out_ap=ap, in_ap=ap, remote_sem=T.sem[sem], local_sem=T.sem.lsem,
+                     pid=a[1], routing_id=a[0], dma_engine_mask=bits(es))
+
+    def w_ap(s, h=None):
+        if h is None:
+            return T.wall[:, WID * s:WID * (s + 1)]
+        return T.wall[:, WID * s + HALF * h:WID * s + HALF * (h + 1)]
+
+    def load_weights(s):
+        g.sync.dma_start(w_ap(s, 0), T.w1[:, :]).then_inc(T.sem["wa%d" % s], 16)
+        g.scalar.dma_start(w_ap(s, 1), T.w2[:, :]).then_inc(T.sem["wb%d" % s], 16)
+
+    def halves(o, c):
+        a = (c // 2 + 7) // 8 * 8
+        return [(o, a), (o + a, c - a)]
+
+    def pipeline(chunks, stages, src0, dst_last, before_first, need):
+        te, ve = g.tensor, g.vector
+        zw = FT * max(c for o, c in chunks)
+        ve.memset(T.zero[:, 0:zw], 0.0).then_inc(T.sem.zs, 1)
+        wait(ve, "v", "zs", 1)
+        steps = sorted(((k + p, -k, k, p) for k in range(len(chunks)) for p in range(2 * len(stages))))
+        for _a, _b, k, p in steps:
+            o, c = chunks[k]
+            i, s = p // 2, stages[p // 2]
+            ps, ts, vs = T["ps%d" % k], "t%d" % k, "v%d" % k
+            if p % 2 == 0:
+                src = src0 if i == 0 else T.act
+                if i == 0:
+                    before_first(k)
+                else:
+                    wait(te, "t", vs, 2 * i)
+                wait(te, "t", "wa%d" % s, need[s][0])
+                for f in range(FT):
+                    te.matmul(ps[:, f * c:(f + 1) * c], T.wall[:, WID * s + 128 * f:WID * s + 128 * (f + 1)],
+                              src[:, o:o + c], True, True).then_inc(T.sem[ts], 1)
+                wait(ve, "v", ts, 2 * FT * i + FT)
+                ve.tensor_tensor(T.hid[:, FT * o:FT * (o + c)], ps[:, 0:FT * c], T.zero[:, 0:FT * c],
+                                 AluOpType.max).then_inc(T.sem[vs], 1)
+            else:
+                dst = dst_last if i == len(stages) - 1 else T.act
+                wait(te, "t", vs, 2 * i + 1)
+                wait(te, "t", "wb%d" % s, need[s][1])
+                for f in range(FT):
+                    te.matmul(ps[:, FT * c:(FT + 1) * c],
+                              T.wall[:, WID * s + HALF + 128 * f:WID * s + HALF + 128 * (f + 1)],
+                              T.hid[:, FT * o + f * c:FT * o + (f + 1) * c],
+                              f == 0, f == FT - 1).then_inc(T.sem[ts], 1)
+                wait(ve, "v", ts, 2 * FT * (i + 1))
+                ve.tensor_copy(dst[:, o:o + c], ps[:, FT * c:(FT + 1) * c]).then_inc(T.sem[vs], 1)
+
+    if core == first:
+        qs = [g.scalar, g.sync]
+        g.sync.dma_start(w_ap(0, 0), T.w1[:, :]).then_inc(T.sem.wa0, 16)
+        for m in range(NB):
+            qs[m % 2].dma_start(T.xin[:, TK * m:TK * (m + 1)], T.x[m]).then_inc(T.sem["xb%d" % m], 16)
+            if m == 0:
+                g.scalar.dma_start(w_ap(0, 1), T.w2[:, :]).then_inc(T.sem.wb0, 16)
+        chunks = halves(offs[0], width[0]) + [(offs[q], width[q]) for q in range(1, len(comp))]
+
+        def blocks_in(k):
+            o, c = chunks[k]
+            for m in range(o // TK, (o + c - 1) // TK + 1):
+                wait(g.tensor, "t", "xb%d" % m, 16)
+
+        pipeline(chunks, [0], T.xin, T.act, blocks_in, {0: (16, 16)})
+        es = engines(a_relay)
+        gwait("v0", 2)
+        gwait("v1", 2)
+        send_one(T.act[:, offs[0]:offs[0] + width[0]], a_relay[0], es[0:8], "ain")
+        for k in range(2, len(chunks)):
+            gwait("v%d" % k, 2)
+        send([transfer(T.act[:, offs[q]:offs[q] + width[q]], [a_relay[q]], es[4 * q:4 * q + 4], "ain")
+              for q in range(1, len(comp))])
+        gwait("lsem", left[0])
+        return
+
+    if core in a_relay:
+        q = a_relay.index(core)
+        gwait("ain", 8 if q == 0 else 4)
+        send_one(T.act[:, offs[q]:offs[q] + width[q]], comp[q], engines([comp[q]]), "ain")
+        gwait("lsem", left[0])
+        return
+
+    if core in w_jobs:
+        s, h, dsts = w_jobs[core]
+        sem = ("wa%d" if h == 0 else "wb%d") % s
+        gwait(sem, 8)
+        send([transfer(w_ap(s, h), dsts, engines(dsts), sem)])
+        gwait("lsem", left[0])
+        return
+
+    if core not in ranks:
+        return
+    s_own = ranks.index(core)
+
+    if core not in comp:
+        load_weights(s_own)
+        es = engines(w_relay[s_own][0] + w_relay[s_own][1])
+        gwait("wa%d" % s_own, 16)
+        gwait("wb%d" % s_own, 16)
+        send([transfer(w_ap(s_own, 0), w_relay[s_own][0], es[0:8], "wa%d" % s_own),
+              transfer(w_ap(s_own, 1), w_relay[s_own][1], es[8:16], "wb%d" % s_own)])
+        gwait("lsem", left[0])
+        return
+
+    q = comp.index(core)
+    load_weights(s_own)
+    others = [d for d in comp if d != core]
+    gwait("wa%d" % s_own, 16)
+    gwait("wb%d" % s_own, 16)
+    send([transfer(w_ap(s_own), others, engines(others), "wa%d" % s_own)])
+
+    need = {}
+    for s in range(1, NST):
+        need[s] = (16, 16) if s == s_own else ((8, 0) if ranks[s] in comp else (8, 8))
+    chunks = halves(offs[q], width[q])
+    stages = list(range(1, NST))
+    pipeline(chunks, stages, T.act, T.out, lambda k: wait(g.tensor, "t", "ain", 8), need)
+    done = 2 * len(stages)
+
+    if core != last:
+        for k in range(len(chunks)):
+            gwait("v%d" % k, done)
+        send_one(T.out[:, offs[q]:offs[q] + width[q]], last, engines([last]), "res%d" % q)
+        gwait("lsem", left[0])
+        return
+
+    def makers(m):
+        w = []
+        for k, (o, c) in enumerate(chunks):
+            if o < TK * (m + 1) and o + c > TK * m:
+                w.append(("v%d" % k, done))
+        for j in range(1, len(comp)):
+            if offs[j] < TK * (m + 1) and offs[j] + width[j] > TK * m:
+                w.append(("res%d" % j, 8))
+        return w
+
+    own = [m for m in range(NB) if all(sem[0] == "v" for sem, val in makers(m))]
+    rest = [m for m in range(NB) if m not in own]
+    cut = (len(rest) + 1) // 2
+    for qu, qn, ms in ((g.sync, "sy", own + rest[cut:]), (g.scalar, "sc", rest[:cut])):
+        for m in ms:
+            for sem, val in makers(m):
+                wait(qu, qn, sem, val)
+            qu.dma_start(T.y[m], T.out[:, TK * m:TK * (m + 1)]).then_inc(T.sem.st, 16)
+    gwait("st", 16 * NB)
+    gwait("lsem", left[0])

@@ -6,8 +6,11 @@ NST = 8
 COLS = NB * TK
 HALF = FT * 128
 WID = 2 * HALF
-C_HELP = 96
-NCH = 5
+NT = 2 * FT
+NCOMP = 4
+SHARE = COLS // NCOMP
+BPS = SHARE // TK
+NCH = 4
 
 SCRATCH = {
     "wall": ("sbuf", [128, NST * WID], "bfloat16"),
@@ -15,16 +18,17 @@ SCRATCH = {
     "act": ("sbuf", [128, COLS], "bfloat16"),
     "hid": ("sbuf", [128, FT * COLS], "bfloat16"),
     "out": ("sbuf", [128, COLS], "bfloat16"),
-    "zero": ("sbuf", [128, 512], "float32"),
+    "zero": ("sbuf", [128, SHARE], "float32"),
+    "ybuf": ("dram", [NB, 128, TK], "bfloat16"),
 }
-for _k in range(NCH):
+for _k in range(2 * NCH):
     SCRATCH["ps%d" % _k] = ("psum", [128, 512], "float32")
 
-SEMAPHORES = (["wa%d" % s for s in range(NST)] + ["wb%d" % s for s in range(NST)]
+SEMAPHORES = (["w%d_%d" % (t, s) for s in range(NST) for t in range(NT)]
               + ["xb%d" % m for m in range(NB)]
-              + ["t%d" % k for k in range(NCH)] + ["v%d" % k for k in range(NCH)]
-              + ["res%d" % q for q in range(1, 4)]
-              + ["ain", "lsem", "st", "zs"])
+              + [n + "%d" % k for k in range(NCH) for n in ("ta", "tb", "va", "vb", "vc")]
+              + ["res%d" % q for q in range(1, NCOMP)]
+              + ["ain", "afw", "lsem", "st", "zs"])
 
 
 def rank_program(g, core, T, topo):
@@ -32,27 +36,43 @@ def rank_program(g, core, T, topo):
     first, last = ranks[0], ranks[-1]
     every = range(topo.CHIPS * topo.CORES_PER_CHIP)
 
-    comp = [last] + [r for r in ranks[1:-1] if topo.may_write(r, last)]
-    width = [COLS - C_HELP * (len(comp) - 1)] + [C_HELP] * (len(comp) - 1)
-    offs = [sum(width[:q]) for q in range(len(comp))]
-
     def port_cores(r):
         c = [k for k in every if topo.chip(k) == topo.chip(r) and k not in ranks
-             and all(topo.may_write(k, d) for d in comp)]
+             and topo.may_write(k, first) and topo.may_write(k, last)]
         return ([k for k in c if topo.die(k) == topo.die(r)], [k for k in c if topo.die(k) != topo.die(r)])
 
-    near, far = port_cores(first)
-    a_relay = [far[0], near[0], far[1], near[1]]
+    cross = [r for r in ranks if not topo.may_write(r, last)]
+    hub = {}
+    for r in cross:
+        hub[r] = port_cores(r)[1][0]
+    comp = [last, hub[cross[1]], hub[cross[2]], hub[cross[0]]]
+    side = comp[1:]
+    offs = [SHARE * q for q in range(NCOMP)]
+
     w_jobs = {}
     w_relay = {}
+    fwd = {}
+    direct = {}
+    second = {}
+    whole = {}
     for s in range(1, NST):
-        if ranks[s] in comp:
-            continue
-        nr, fr = port_cores(ranks[s])
-        w_relay[s] = [[fr[0], nr[1]], [nr[0], fr[1]]]
-        for h in range(2):
-            for p in range(2):
-                w_jobs[w_relay[s][h][p]] = (s, h, comp[2 * p:2 * p + 2])
+        r = ranks[s]
+        if r in cross:
+            extra = side[cross.index(r) % len(side)]
+            direct[s] = [d for d in side if d != hub[r] and d != extra]
+            if hub[r] in comp:
+                second[s] = port_cores(r)[1][1]
+                fwd[hub[r]] = (s, [last], 8)
+                fwd[second[s]] = (s, [extra], 4)
+            else:
+                fwd[hub[r]] = (s, [last, extra], 8)
+            for d in comp:
+                whole[(s, d)] = 4 if (s in second and d in direct[s]) else 8
+        else:
+            nr, fr = port_cores(r)
+            w_relay[s] = [fr[0], nr[0], nr[1], fr[1]]
+            for t in range(NT):
+                w_jobs[w_relay[s][t]] = (s, t)
 
     waited = {}
     left = [0]
@@ -64,6 +84,9 @@ def rank_program(g, core, T, topo):
 
     def gwait(sem, val):
         wait(g, "g", sem, val)
+
+    def ws(t, s):
+        return "w%d_%d" % (t, s)
 
     def engines(dsts):
         m = topo.mask(core, dsts[0])
@@ -77,14 +100,14 @@ def rank_program(g, core, T, topo):
             m |= 1 << e
         return m
 
-    def transfer(ap, dsts, es, sem):
+    def transfer(src, dsts, es, sem, dst=None):
         ids = []
         for d in dsts:
             a = topo.addr(d)
             ids.append(DstId(rid=a[0], pnc=a[1]))
         left[0] += len(es)
         return RemoteDMATransfer(dst_ids=ids, dma_engine_mask=bits(es), remote_sem=T.sem[sem],
-                                 srcs=[ap], dsts=[ap for d in dsts], alu_op=0)
+                                 srcs=[src], dsts=[(src if dst is None else dst) for d in dsts], alu_op=0)
 
     def send(trs):
         g.remote_dma_fused(trs, local_sem=T.sem.lsem)
@@ -95,148 +118,173 @@ def rank_program(g, core, T, topo):
         g.remote_dma(out_ap=ap, in_ap=ap, remote_sem=T.sem[sem], local_sem=T.sem.lsem,
                      pid=a[1], routing_id=a[0], dma_engine_mask=bits(es))
 
-    def w_ap(s, h=None):
-        if h is None:
-            return T.wall[:, WID * s:WID * (s + 1)]
-        return T.wall[:, WID * s + HALF * h:WID * s + HALF * (h + 1)]
+    def w_ap(s):
+        return T.wall[:, WID * s:WID * (s + 1)]
+
+    def tile(s, t):
+        return T.wall[:, WID * s + 128 * t:WID * s + 128 * (t + 1)]
+
+    def share_ap(buf, q):
+        return buf[:, offs[q]:offs[q] + SHARE]
 
     def load_weights(s):
-        g.sync.dma_start(w_ap(s, 0), T.w1[:, :]).then_inc(T.sem["wa%d" % s], 16)
-        g.scalar.dma_start(w_ap(s, 1), T.w2[:, :]).then_inc(T.sem["wb%d" % s], 16)
+        g.sync.dma_start(T.wall[:, WID * s:WID * s + HALF], T.w1[:, :]).then_inc(T.sem[ws(0, s)], 16)
+        g.scalar.dma_start(T.wall[:, WID * s + HALF:WID * (s + 1)], T.w2[:, :]).then_inc(T.sem[ws(2, s)], 16)
 
-    def halves(o, c):
-        a = (c // 2 + 7) // 8 * 8
-        return [(o, a), (o + a, c - a)]
+    def loaded(s):
+        gwait(ws(0, s), 16)
+        gwait(ws(2, s), 16)
 
-    def pipeline(chunks, stages, src0, dst_last, before_first, need):
+    def tiles_out(s):
+        es = engines(w_relay[s])
+        per = len(es) // NT
+        send([transfer(tile(s, t), [w_relay[s][t]], es[per * t:per * (t + 1)], ws(t, s)) for t in range(NT)])
+        return per
+
+    def pipeline(chunks, stages, src0, dst_last, before_first, need, one_by_one):
         te, ve = g.tensor, g.vector
-        zw = FT * max(c for o, c in chunks)
+        zw = max(c for o, c in chunks)
         ve.memset(T.zero[:, 0:zw], 0.0).then_inc(T.sem.zs, 1)
         wait(ve, "v", "zs", 1)
-        steps = sorted(((k + p, -k, k, p) for k in range(len(chunks)) for p in range(2 * len(stages))))
+        steps = sorted(((k + p, (k if one_by_one else -k), k, p)
+                        for k in range(len(chunks)) for p in range(2 * len(stages))))
         for _a, _b, k, p in steps:
             o, c = chunks[k]
             i, s = p // 2, stages[p // 2]
-            ps, ts, vs = T["ps%d" % k], "t%d" % k, "v%d" % k
+            pa, pb = T["ps%d" % (2 * k)], T["ps%d" % (2 * k + 1)]
+            ta, tb, va, vb, vc = ["%s%d" % (n, k) for n in ("ta", "tb", "va", "vb", "vc")]
+            h0 = T.hid[:, FT * o:FT * o + c]
+            h1 = T.hid[:, FT * o + c:FT * o + 2 * c]
             if p % 2 == 0:
                 src = src0 if i == 0 else T.act
                 if i == 0:
                     before_first(k)
                 else:
-                    wait(te, "t", vs, 2 * i)
-                wait(te, "t", "wa%d" % s, need[s][0])
-                for f in range(FT):
-                    te.matmul(ps[:, f * c:(f + 1) * c], T.wall[:, WID * s + 128 * f:WID * s + 128 * (f + 1)],
-                              src[:, o:o + c], True, True).then_inc(T.sem[ts], 1)
-                wait(ve, "v", ts, 2 * FT * i + FT)
-                ve.tensor_tensor(T.hid[:, FT * o:FT * (o + c)], ps[:, 0:FT * c], T.zero[:, 0:FT * c],
-                                 AluOpType.max).then_inc(T.sem[vs], 1)
+                    wait(te, "t", vc, i)
+                wait(te, "t", ws(0, s), need[s][0])
+                te.matmul(pa[:, 0:c], tile(s, 0), src[:, o:o + c], True, True).then_inc(T.sem[ta], 1)
+                wait(te, "t", ws(1, s), need[s][1])
+                te.matmul(pb[:, 0:c], tile(s, 1), src[:, o:o + c], True, True).then_inc(T.sem[tb], 1)
+                wait(ve, "v", ta, 2 * i + 1)
+                ve.tensor_tensor(h0, pa[:, 0:c], T.zero[:, 0:c], AluOpType.max).then_inc(T.sem[va], 1)
+                wait(ve, "v", tb, 2 * i + 1)
+                ve.tensor_tensor(h1, pb[:, 0:c], T.zero[:, 0:c], AluOpType.max).then_inc(T.sem[vb], 1)
             else:
                 dst = dst_last if i == len(stages) - 1 else T.act
-                wait(te, "t", vs, 2 * i + 1)
-                wait(te, "t", "wb%d" % s, need[s][1])
-                for f in range(FT):
-                    te.matmul(ps[:, FT * c:(FT + 1) * c],
-                              T.wall[:, WID * s + HALF + 128 * f:WID * s + HALF + 128 * (f + 1)],
-                              T.hid[:, FT * o + f * c:FT * o + (f + 1) * c],
-                              f == 0, f == FT - 1).then_inc(T.sem[ts], 1)
-                wait(ve, "v", ts, 2 * FT * (i + 1))
-                ve.tensor_copy(dst[:, o:o + c], ps[:, FT * c:(FT + 1) * c]).then_inc(T.sem[vs], 1)
+                wait(te, "t", ws(2, s), need[s][2])
+                wait(te, "t", ws(3, s), need[s][3])
+                wait(te, "t", va, i + 1)
+                te.matmul(pa[:, c:2 * c], tile(s, 2), h0, True, False).then_inc(T.sem[ta], 1)
+                wait(te, "t", vb, i + 1)
+                te.matmul(pa[:, c:2 * c], tile(s, 3), h1, False, True).then_inc(T.sem[tb], 1)
+                wait(ve, "v", ta, 2 * i + 2)
+                wait(ve, "v", tb, 2 * i + 2)
+                ve.tensor_copy(dst[:, o:o + c], pa[:, c:2 * c]).then_inc(T.sem[vc], 1)
 
     if core == first:
         qs = [g.scalar, g.sync]
-        g.sync.dma_start(w_ap(0, 0), T.w1[:, :]).then_inc(T.sem.wa0, 16)
+        g.sync.dma_start(T.wall[:, 0:HALF], T.w1[:, :]).then_inc(T.sem[ws(0, 0)], 16)
         for m in range(NB):
             qs[m % 2].dma_start(T.xin[:, TK * m:TK * (m + 1)], T.x[m]).then_inc(T.sem["xb%d" % m], 16)
             if m == 0:
-                g.scalar.dma_start(w_ap(0, 1), T.w2[:, :]).then_inc(T.sem.wb0, 16)
-        chunks = halves(offs[0], width[0]) + [(offs[q], width[q]) for q in range(1, len(comp))]
+                g.scalar.dma_start(T.wall[:, HALF:WID], T.w2[:, :]).then_inc(T.sem[ws(2, 0)], 16)
+        chunks = [(offs[q], SHARE) for q in range(NCOMP)]
 
         def blocks_in(k):
-            o, c = chunks[k]
-            for m in range(o // TK, (o + c - 1) // TK + 1):
+            for m in range(BPS * k, BPS * (k + 1)):
                 wait(g.tensor, "t", "xb%d" % m, 16)
 
-        pipeline(chunks, [0], T.xin, T.act, blocks_in, {0: (16, 16)})
-        es = engines(a_relay)
-        gwait("v0", 2)
-        gwait("v1", 2)
-        send_one(T.act[:, offs[0]:offs[0] + width[0]], a_relay[0], es[0:8], "ain")
-        for k in range(2, len(chunks)):
-            gwait("v%d" % k, 2)
-        send([transfer(T.act[:, offs[q]:offs[q] + width[q]], [a_relay[q]], es[4 * q:4 * q + 4], "ain")
-              for q in range(1, len(comp))])
-        gwait("lsem", left[0])
-        return
-
-    if core in a_relay:
-        q = a_relay.index(core)
-        gwait("ain", 8 if q == 0 else 4)
-        send_one(T.act[:, offs[q]:offs[q] + width[q]], comp[q], engines([comp[q]]), "ain")
+        pipeline(chunks, [0], T.xin, T.act, blocks_in, {0: (16, 0, 16, 0)}, True)
+        off = engines(side)
+        on = [e for e in engines([comp[3]]) if e not in off][:8]
+        gwait("vc0", 1)
+        send_one(share_ap(T.act, 0), comp[3], on, "afw")
+        gwait("vc1", 1)
+        send_one(share_ap(T.act, 1), comp[1], off, "ain")
+        gwait("vc2", 1)
+        send_one(share_ap(T.act, 2), comp[2], off, "ain")
+        gwait("vc3", 1)
+        send_one(share_ap(T.act, 3), comp[3], on, "ain")
         gwait("lsem", left[0])
         return
 
     if core in w_jobs:
-        s, h, dsts = w_jobs[core]
-        sem = ("wa%d" if h == 0 else "wb%d") % s
-        gwait(sem, 8)
-        send([transfer(w_ap(s, h), dsts, engines(dsts), sem)])
+        s, t = w_jobs[core]
+        gwait(ws(t, s), 4)
+        send([transfer(tile(s, t), side, engines(side), ws(t, s))])
         gwait("lsem", left[0])
         return
 
-    if core not in ranks:
+    if core in ranks and core != last:
+        s = ranks.index(core)
+        load_weights(s)
+        loaded(s)
+        if core in cross:
+            off = engines(direct[s])
+            on = [e for e in engines([hub[core]]) if e not in off][:8]
+            if s in second:
+                send([transfer(w_ap(s), [hub[core]], on, ws(0, s)),
+                      transfer(w_ap(s), [second[s]], off[4:8], ws(0, s)),
+                      transfer(w_ap(s), direct[s], off[0:4], ws(0, s))])
+            else:
+                send([transfer(w_ap(s), [hub[core]], on, ws(0, s)),
+                      transfer(w_ap(s), direct[s], off, ws(0, s))])
+        else:
+            tiles_out(s)
+            send_one(w_ap(s), last, engines([last]), ws(0, s))
+        gwait("lsem", left[0])
         return
-    s_own = ranks.index(core)
 
+    if core not in comp and core not in fwd:
+        return
+
+    if core == comp[3]:
+        gwait("afw", 8)
+        send_one(share_ap(T.act, 0), last, engines([last]), "ain")
+    if core in fwd:
+        s, dsts, got = fwd[core]
+        gwait(ws(0, s), got)
+        send([transfer(w_ap(s), dsts, engines(dsts), ws(0, s))])
     if core not in comp:
-        load_weights(s_own)
-        es = engines(w_relay[s_own][0] + w_relay[s_own][1])
-        gwait("wa%d" % s_own, 16)
-        gwait("wb%d" % s_own, 16)
-        send([transfer(w_ap(s_own, 0), w_relay[s_own][0], es[0:8], "wa%d" % s_own),
-              transfer(w_ap(s_own, 1), w_relay[s_own][1], es[8:16], "wb%d" % s_own)])
         gwait("lsem", left[0])
         return
 
     q = comp.index(core)
-    load_weights(s_own)
-    others = [d for d in comp if d != core]
-    gwait("wa%d" % s_own, 16)
-    gwait("wb%d" % s_own, 16)
-    send([transfer(w_ap(s_own), others, engines(others), "wa%d" % s_own)])
+    if core == last:
+        load_weights(NST - 1)
+        loaded(NST - 1)
+        tiles_out(NST - 1)
 
     need = {}
     for s in range(1, NST):
-        need[s] = (16, 16) if s == s_own else ((8, 0) if ranks[s] in comp else (8, 8))
-    chunks = halves(offs[q], width[q])
+        if ranks[s] == core:
+            need[s] = (16, 0, 16, 0)
+        elif ranks[s] in cross:
+            need[s] = (whole[(s, core)], 0, 0, 0)
+        elif core == last:
+            need[s] = (8, 0, 0, 0)
+        else:
+            need[s] = (8, 8, 8, 8)
+    chunks = [(offs[q] + TK * j, TK) for j in range(BPS)]
     stages = list(range(1, NST))
-    pipeline(chunks, stages, T.act, T.out, lambda k: wait(g.tensor, "t", "ain", 8), need)
-    done = 2 * len(stages)
+    pipeline(chunks, stages, T.act, T.out, lambda k: wait(g.tensor, "t", "ain", 8), need, False)
+    done = len(stages)
 
     if core != last:
-        for k in range(len(chunks)):
-            gwait("v%d" % k, done)
-        send_one(T.out[:, offs[q]:offs[q] + width[q]], last, engines([last]), "res%d" % q)
+        es = engines([last])
+        per = len(es) // BPS
+        for j in range(BPS):
+            gwait("vc%d" % j, done)
+        send([transfer(T.out[:, offs[q] + TK * j:offs[q] + TK * (j + 1)], [last], es[per * j:per * (j + 1)],
+                       "res%d" % q, T.ybuf[BPS * q + j]) for j in range(BPS)])
         gwait("lsem", left[0])
         return
 
-    def makers(m):
-        w = []
-        for k, (o, c) in enumerate(chunks):
-            if o < TK * (m + 1) and o + c > TK * m:
-                w.append(("v%d" % k, done))
-        for j in range(1, len(comp)):
-            if offs[j] < TK * (m + 1) and offs[j] + width[j] > TK * m:
-                w.append(("res%d" % j, 8))
-        return w
-
-    own = [m for m in range(NB) if all(sem[0] == "v" for sem, val in makers(m))]
-    rest = [m for m in range(NB) if m not in own]
-    cut = (len(rest) + 1) // 2
-    for qu, qn, ms in ((g.sync, "sy", own + rest[cut:]), (g.scalar, "sc", rest[:cut])):
-        for m in ms:
-            for sem, val in makers(m):
-                wait(qu, qn, sem, val)
-            qu.dma_start(T.y[m], T.out[:, TK * m:TK * (m + 1)]).then_inc(T.sem.st, 16)
-    gwait("st", 16 * NB)
+    for j in range(BPS):
+        wait(g.sync, "sy", "vc%d" % j, done)
+        g.sync.dma_start(T.y[j], T.out[:, TK * j:TK * (j + 1)]).then_inc(T.sem.st, 16)
+    for p in range(1, NCOMP):
+        wait(g.scalar, "sc", "res%d" % p, 8)
+        g.scalar.dma_start(T.y[BPS * p:BPS * (p + 1)], T.ybuf[BPS * p:BPS * (p + 1)]).then_inc(T.sem.st, 16)
+    gwait("st", 16 * (BPS + NCOMP - 1))
     gwait("lsem", left[0])

from concourse.bass import DstId, RemoteDMATransfer
from concourse.mybir import AluOpType

NB, TK, FT = 8, 64, 2
NST = 8
COLS = NB * TK
HALF = FT * 128
WID = 2 * HALF
NT = 2 * FT
NCOMP = 4
SHARE = COLS // NCOMP
BPS = SHARE // TK
NCH = 4

SCRATCH = {
    "wall": ("sbuf", [128, NST * WID], "bfloat16"),
    "xin": ("sbuf", [128, COLS], "bfloat16"),
    "act": ("sbuf", [128, COLS], "bfloat16"),
    "hid": ("sbuf", [128, FT * COLS], "bfloat16"),
    "out": ("sbuf", [128, COLS], "bfloat16"),
    "zero": ("sbuf", [128, SHARE], "float32"),
    "ybuf": ("dram", [NB, 128, TK], "bfloat16"),
}
for _k in range(2 * NCH):
    SCRATCH["ps%d" % _k] = ("psum", [128, 512], "float32")

SEMAPHORES = (["w%d_%d" % (t, s) for s in range(NST) for t in range(NT)]
              + ["xb%d" % m for m in range(NB)]
              + [n + "%d" % k for k in range(NCH) for n in ("ta", "tb", "va", "vb", "vc")]
              + ["res%d" % q for q in range(1, NCOMP)]
              + ["ain", "afw", "lsem", "st", "zs"])


def rank_program(g, core, T, topo):
    ranks = list(T.cores)
    first, last = ranks[0], ranks[-1]
    every = range(topo.CHIPS * topo.CORES_PER_CHIP)

    def port_cores(r):
        c = [k for k in every if topo.chip(k) == topo.chip(r) and k not in ranks
             and topo.may_write(k, first) and topo.may_write(k, last)]
        return ([k for k in c if topo.die(k) == topo.die(r)], [k for k in c if topo.die(k) != topo.die(r)])

    cross = [r for r in ranks if not topo.may_write(r, last)]
    hub = {}
    for r in cross:
        hub[r] = port_cores(r)[1][0]
    comp = [last, hub[cross[1]], hub[cross[2]], hub[cross[0]]]
    side = comp[1:]
    offs = [SHARE * q for q in range(NCOMP)]

    w_jobs = {}
    w_relay = {}
    fwd = {}
    direct = {}
    second = {}
    whole = {}
    for s in range(1, NST):
        r = ranks[s]
        if r in cross:
            extra = side[cross.index(r) % len(side)]
            direct[s] = [d for d in side if d != hub[r] and d != extra]
            if hub[r] in comp:
                second[s] = port_cores(r)[1][1]
                fwd[hub[r]] = (s, [last], 8)
                fwd[second[s]] = (s, [extra], 4)
            else:
                fwd[hub[r]] = (s, [last, extra], 8)
            for d in comp:
                whole[(s, d)] = 4 if (s in second and d in direct[s]) else 8
        else:
            nr, fr = port_cores(r)
            w_relay[s] = [fr[0], nr[0], nr[1], fr[1]]
            for t in range(NT):
                w_jobs[w_relay[s][t]] = (s, t)

    waited = {}
    left = [0]

    def wait(q, qname, sem, val):
        if val > waited.get((qname, sem), 0):
            waited[(qname, sem)] = val
            q.wait_ge(T.sem[sem], val)

    def gwait(sem, val):
        wait(g, "g", sem, val)

    def ws(t, s):
        return "w%d_%d" % (t, s)

    def engines(dsts):
        m = topo.mask(core, dsts[0])
        for d in dsts[1:]:
            m &= topo.mask(core, d)
        return [e for e in range(m.bit_length()) if (m >> e) & 1]

    def bits(es):
        m = 0
        for e in es:
            m |= 1 << e
        return m

    def transfer(src, dsts, es, sem, dst=None):
        ids = []
        for d in dsts:
            a = topo.addr(d)
            ids.append(DstId(rid=a[0], pnc=a[1]))
        left[0] += len(es)
        return RemoteDMATransfer(dst_ids=ids, dma_engine_mask=bits(es), remote_sem=T.sem[sem],
                                 srcs=[src], dsts=[(src if dst is None else dst) for d in dsts], alu_op=0)

    def send(trs):
        g.remote_dma_fused(trs, local_sem=T.sem.lsem)

    def send_one(ap, dst, es, sem):
        a = topo.addr(dst)
        left[0] += len(es)
        g.remote_dma(out_ap=ap, in_ap=ap, remote_sem=T.sem[sem], local_sem=T.sem.lsem,
                     pid=a[1], routing_id=a[0], dma_engine_mask=bits(es))

    def w_ap(s):
        return T.wall[:, WID * s:WID * (s + 1)]

    def tile(s, t):
        return T.wall[:, WID * s + 128 * t:WID * s + 128 * (t + 1)]

    def share_ap(buf, q):
        return buf[:, offs[q]:offs[q] + SHARE]

    def load_weights(s):
        g.sync.dma_start(T.wall[:, WID * s:WID * s + HALF], T.w1[:, :]).then_inc(T.sem[ws(0, s)], 16)
        g.scalar.dma_start(T.wall[:, WID * s + HALF:WID * (s + 1)], T.w2[:, :]).then_inc(T.sem[ws(2, s)], 16)

    def loaded(s):
        gwait(ws(0, s), 16)
        gwait(ws(2, s), 16)

    def tiles_out(s):
        es = engines(w_relay[s])
        per = len(es) // NT
        send([transfer(tile(s, t), [w_relay[s][t]], es[per * t:per * (t + 1)], ws(t, s)) for t in range(NT)])
        return per

    def pipeline(chunks, stages, src0, dst_last, before_first, need, one_by_one):
        te, ve = g.tensor, g.vector
        zw = max(c for o, c in chunks)
        ve.memset(T.zero[:, 0:zw], 0.0).then_inc(T.sem.zs, 1)
        wait(ve, "v", "zs", 1)
        steps = sorted(((k + p, (k if one_by_one else -k), k, p)
                        for k in range(len(chunks)) for p in range(2 * len(stages))))
        for _a, _b, k, p in steps:
            o, c = chunks[k]
            i, s = p // 2, stages[p // 2]
            pa, pb = T["ps%d" % (2 * k)], T["ps%d" % (2 * k + 1)]
            ta, tb, va, vb, vc = ["%s%d" % (n, k) for n in ("ta", "tb", "va", "vb", "vc")]
            h0 = T.hid[:, FT * o:FT * o + c]
            h1 = T.hid[:, FT * o + c:FT * o + 2 * c]
            if p % 2 == 0:
                src = src0 if i == 0 else T.act
                if i == 0:
                    before_first(k)
                else:
                    wait(te, "t", vc, i)
                wait(te, "t", ws(0, s), need[s][0])
                te.matmul(pa[:, 0:c], tile(s, 0), src[:, o:o + c], True, True).then_inc(T.sem[ta], 1)
                wait(te, "t", ws(1, s), need[s][1])
                te.matmul(pb[:, 0:c], tile(s, 1), src[:, o:o + c], True, True).then_inc(T.sem[tb], 1)
                wait(ve, "v", ta, 2 * i + 1)
                ve.tensor_tensor(h0, pa[:, 0:c], T.zero[:, 0:c], AluOpType.max).then_inc(T.sem[va], 1)
                wait(ve, "v", tb, 2 * i + 1)
                ve.tensor_tensor(h1, pb[:, 0:c], T.zero[:, 0:c], AluOpType.max).then_inc(T.sem[vb], 1)
            else:
                dst = dst_last if i == len(stages) - 1 else T.act
                wait(te, "t", ws(2, s), need[s][2])
                wait(te, "t", ws(3, s), need[s][3])
                wait(te, "t", va, i + 1)
                te.matmul(pa[:, c:2 * c], tile(s, 2), h0, True, False).then_inc(T.sem[ta], 1)
                wait(te, "t", vb, i + 1)
                te.matmul(pa[:, c:2 * c], tile(s, 3), h1, False, True).then_inc(T.sem[tb], 1)
                wait(ve, "v", ta, 2 * i + 2)
                wait(ve, "v", tb, 2 * i + 2)
                ve.tensor_copy(dst[:, o:o + c], pa[:, c:2 * c]).then_inc(T.sem[vc], 1)

    if core == first:
        qs = [g.scalar, g.sync]
        g.sync.dma_start(T.wall[:, 0:HALF], T.w1[:, :]).then_inc(T.sem[ws(0, 0)], 16)
        for m in range(NB):
            qs[m % 2].dma_start(T.xin[:, TK * m:TK * (m + 1)], T.x[m]).then_inc(T.sem["xb%d" % m], 16)
            if m == 0:
                g.scalar.dma_start(T.wall[:, HALF:WID], T.w2[:, :]).then_inc(T.sem[ws(2, 0)], 16)
        chunks = [(offs[q], SHARE) for q in range(NCOMP)]

        def blocks_in(k):
            for m in range(BPS * k, BPS * (k + 1)):
                wait(g.tensor, "t", "xb%d" % m, 16)

        pipeline(chunks, [0], T.xin, T.act, blocks_in, {0: (16, 0, 16, 0)}, True)
        off = engines(side)
        on = [e for e in engines([comp[3]]) if e not in off][:8]
        gwait("vc0", 1)
        send_one(share_ap(T.act, 0), comp[3], on, "afw")
        gwait("vc1", 1)
        send_one(share_ap(T.act, 1), comp[1], off, "ain")
        gwait("vc2", 1)
        send_one(share_ap(T.act, 2), comp[2], off, "ain")
        gwait("vc3", 1)
        send_one(share_ap(T.act, 3), comp[3], on, "ain")
        gwait("lsem", left[0])
        return

    if core in w_jobs:
        s, t = w_jobs[core]
        gwait(ws(t, s), 4)
        send([transfer(tile(s, t), side, engines(side), ws(t, s))])
        gwait("lsem", left[0])
        return

    if core in ranks and core != last:
        s = ranks.index(core)
        load_weights(s)
        loaded(s)
        if core in cross:
            off = engines(direct[s])
            on = [e for e in engines([hub[core]]) if e not in off][:8]
            if s in second:
                send([transfer(w_ap(s), [hub[core]], on, ws(0, s)),
                      transfer(w_ap(s), [second[s]], off[4:8], ws(0, s)),
                      transfer(w_ap(s), direct[s], off[0:4], ws(0, s))])
            else:
                send([transfer(w_ap(s), [hub[core]], on, ws(0, s)),
                      transfer(w_ap(s), direct[s], off, ws(0, s))])
        else:
            tiles_out(s)
            send_one(w_ap(s), last, engines([last]), ws(0, s))
        gwait("lsem", left[0])
        return

    if core not in comp and core not in fwd:
        return

    if core == comp[3]:
        gwait("afw", 8)
        send_one(share_ap(T.act, 0), last, engines([last]), "ain")
    if core in fwd:
        s, dsts, got = fwd[core]
        gwait(ws(0, s), got)
        send([transfer(w_ap(s), dsts, engines(dsts), ws(0, s))])
    if core not in comp:
        gwait("lsem", left[0])
        return

    q = comp.index(core)
    if core == last:
        load_weights(NST - 1)
        loaded(NST - 1)
        tiles_out(NST - 1)

    need = {}
    for s in range(1, NST):
        if ranks[s] == core:
            need[s] = (16, 0, 16, 0)
        elif ranks[s] in cross:
            need[s] = (whole[(s, core)], 0, 0, 0)
        elif core == last:
            need[s] = (8, 0, 0, 0)
        else:
            need[s] = (8, 8, 8, 8)
    chunks = [(offs[q] + TK * j, TK) for j in range(BPS)]
    stages = list(range(1, NST))
    pipeline(chunks, stages, T.act, T.out, lambda k: wait(g.tensor, "t", "ain", 8), need, False)
    done = len(stages)

    if core != last:
        es = engines([last])
        per = len(es) // BPS
        for j in range(BPS):
            gwait("vc%d" % j, done)
        send([transfer(T.out[:, offs[q] + TK * j:offs[q] + TK * (j + 1)], [last], es[per * j:per * (j + 1)],
                       "res%d" % q, T.ybuf[BPS * q + j]) for j in range(BPS)])
        gwait("lsem", left[0])
        return

    for j in range(BPS):
        wait(g.sync, "sy", "vc%d" % j, done)
        g.sync.dma_start(T.y[j], T.out[:, TK * j:TK * (j + 1)]).then_inc(T.sem.st, 16)
    for p in range(1, NCOMP):
        wait(g.scalar, "sc", "res%d" % p, 8)
        g.scalar.dma_start(T.y[BPS * p:BPS * (p + 1)], T.ybuf[BPS * p:BPS * (p + 1)]).then_inc(T.sem.st, 16)
    gwait("st", 16 * (BPS + NCOMP - 1))
    gwait("lsem", left[0])
